import numpy as np
import ml_dtypes


def mxq(x, axis, fmt="e4m3"):
    dtype, down = {"e4m3": (ml_dtypes.float8_e4m3fn, 7), "e5m2": (ml_dtypes.float8_e5m2, 14)}[fmt]
    v = np.moveaxis(np.asarray(x, np.float32).astype(ml_dtypes.bfloat16).astype(np.float64), axis, -1)
    blocks = v.reshape(v.shape[:-1] + (-1, 32))
    amax = np.abs(blocks).max(-1, keepdims=True)
    byte = np.maximum(np.where(amax > 0, np.frexp(amax)[1] - 1 + 127, 0) - down, 1)
    scale = np.exp2(byte - 127.0)
    codes = (blocks / scale).astype(np.float32).astype(dtype).astype(np.float64)
    return np.moveaxis((codes * scale).reshape(v.shape), -1, axis)


WIDE = False


def mx_kscale(k):
    if not WIDE:
        return np.ones(k)
    levels = np.array([10, -10, 5, -5, 0])
    if k % 512:
        return np.exp2(np.random.permutation(np.resize(levels, k // 32))).repeat(32)
    a = np.empty((k // 512, 16))
    for p in range(k // 512):
        a[p, :8] = np.random.permutation(np.resize(levels, 8))
        for g in range(8):
            far = levels[np.abs(levels - a[p, g]) >= 10]
            a[p, g + 8] = far[np.random.randint(len(far))]
    return np.exp2(a.ravel()).repeat(32)


def f64(x):
    return np.asarray(x).astype(np.float64)


def striped(idx):
    return np.tile(idx.reshape(-1, 16).T, (8, 1)).astype(np.uint16)


def unstriped(offs):
    return offs[:16].T.reshape(-1).astype(np.int64)


def striped8(idx):
    return np.concatenate([x.reshape(-1, 16).T for x in idx]).astype(np.uint16)


def runs(offs, k):
    lists = np.stack([offs[16 * r : 16 * r + 16].T.reshape(-1) for r in range(8)]).astype(np.int64)
    return lists[np.arange(k) % 512 // 64]


def pack_weight(w):
    k, n = w.shape
    w = f64(np.asarray(w, np.float32).astype(ml_dtypes.bfloat16)).reshape(k // 32, 32, n)
    amax = np.abs(w).max(1)
    byte = np.clip(np.where(amax > 0, np.frexp(amax)[1] - 1 + 127 - 7, 1), 1, 254)
    scaled = (w * np.exp2(127.0 - byte)[:, None, :]).reshape(k, n).astype(np.float32)
    words = np.ascontiguousarray(scaled.reshape(k // 512, 128, 4, n).transpose(0, 1, 3, 2)).astype(ml_dtypes.float8_e4m3fn).view(np.uint8)
    return words, np.ascontiguousarray(byte.astype(np.uint8).reshape(k // 512, 16, n))


def unpack_weight(words, scales):
    g, p, n, _ = words.shape
    vals = np.ascontiguousarray(words).view(ml_dtypes.float8_e4m3fn).astype(np.float64) * np.repeat(np.exp2(scales.astype(np.float64) - 127.0), 8, axis=1)[..., None]
    return vals.transpose(0, 1, 3, 2).reshape(g * 512, n)


def gelu(v):
    return 0.5 * v * (1.0 + np.tanh(np.sqrt(2.0 / np.pi) * (v + 0.044715 * v**3)))

def planes(y):
    n, m = y.shape
    v = y.astype(np.float32).astype(ml_dtypes.bfloat16).astype(np.float64).reshape(n // 32, 32, m)
    top = np.abs(v).max(1)
    byte = np.clip(np.where(top > 0, np.frexp(top)[1] - 1 + 127 - 7, 1), 1, 254)
    codes = (v * np.exp2(127.0 - byte)[:, None, :]).reshape(n, m).astype(np.float32).astype(ml_dtypes.float8_e4m3fn).view(np.uint8)
    words = codes.reshape(n // 512, 128, 4, m).transpose(0, 1, 3, 2)
    return np.ascontiguousarray(words), np.ascontiguousarray(byte.astype(np.uint8).reshape(n // 512, 16, m))


K, T, S, N, G, H = 512, 2048, 512, 512, 2048, 512


def setup_inputs():
    n = np.random.standard_normal
    s = mx_kscale(K)[:, None]
    u = mx_kscale(H)
    packed_xT = pack_weight(n((K, T)) * s)
    packed_dT = pack_weight(n((K, G)) / s)
    packed_w2 = pack_weight(n((H, N)) / np.sqrt(H) / u[:, None])
    return {
        "x_words": packed_xT[0],
        "x_scales": packed_xT[1],
        "d_words": packed_dT[0],
        "d_scales": packed_dT[1],
        "gn": (np.random.uniform(0.5, 1.5, (H, 1)) * u[:, None]).astype(np.float32),
        "w1": (n((H, H)) / np.sqrt(H) / u[:, None] * u).astype(np.float32),
        "res": (2 * n((N, S))).astype(np.float32),
        "w2_words": packed_w2[0],
        "w2_scales": packed_w2[1],
        "offs": striped(np.random.permutation(T)[:S]),
        "kidx": striped8(np.random.randint(0, G, (8, H))),
        "nb": striped8(np.stack([np.random.permutation(S) for _ in range(8)])),
    }


def reference(x_words, x_scales, d_words, d_scales, gn, w1, res, w2_words, w2_scales, offs, kidx, nb):
    d_kidx = unpack_weight(d_words, d_scales)[np.arange(K)[:, None], runs(kidx, K)]
    xq = unpack_weight(x_words, x_scales)[:, unstriped(offs)]
    s = 0.0625 * (d_kidx.T @ xq)
    z = f64(gn) * s
    h = gelu(mxq(f64(w1), 0, "e4m3").T @ mxq(z, 0, "e4m3"))
    z2 = h + h[np.arange(H)[:, None], runs(nb, H)]
    out_0 = f64(res) + (unpack_weight(w2_words, w2_scales).T @ mxq(z2, 0, "e4m3"))
    return (out_0,) + planes(out_0)

@@ -1,0 +1,242 @@
+from contextlib import ExitStack
+
+import concourse.mybir as mybir
+
+F32 = mybir.dt.float32
+BF16 = mybir.dt.bfloat16
+I32 = mybir.dt.int32
+U32 = mybir.dt.uint32
+U16 = mybir.dt.uint16
+U8 = mybir.dt.uint8
+FP8X4 = mybir.dt.float8_e4m3fn_x4
+MULT = mybir.AluOpType.mult
+ADD = mybir.AluOpType.add
+GELU = mybir.ActivationFunctionType.Gelu_apprx_tanh
+
+P = 128
+PACK = 4
+TABLE = 2048
+S = 512
+HALF = 256
+CHUNK = 128
+CHUNKS = S // CHUNK
+LIST_ROWS = 16
+FLOPS = 3 * 2 * 512 * 512 * 512
+
+
+def tile_picked_scoremlp_gelu_po_kernel(
+    tc, x_words, x_scales, d_words, d_scales, gn, w1, res, w2_words, w2_scales, offs, kidx, nb, out_0, out_1, out_2
+):
+    nc = tc.nc
+    with ExitStack() as ctx:
+        keep = ctx.enter_context(tc.tile_pool(name="keep", bufs=1))
+        reuse = ctx.enter_context(tc.tile_pool(name="reuse", bufs=1))
+        psum = ctx.enter_context(tc.psum_pool(name="psum", bufs=1))
+
+        def sb(name, shape, dtype, tag=None):
+            return keep.tile(shape, dtype, name=name, tag=tag or name, align_bytes=64)
+
+        def at(name, shape, dtype, offset):
+            return reuse.tile(shape, dtype, name=name, align_bytes=64, offset=offset)
+
+        def words_of(packed):
+            return packed[0].rearrange("p n t -> p (n t)").bitcast(I32)
+
+        def deal(dealt, plain):
+            nc.vector.tensor_copy(
+                dealt.rearrange("p (t m) -> p m t", t=PACK), plain.rearrange("p (m t) -> p m t", t=PACK)
+            )
+
+        def cols(c, width):
+            return slice(c * width, (c + 1) * width)
+
+        def entries(lists, c, width):
+            return lists[:, cols(c, width // LIST_ROWS)]
+
+        offs_sb = sb("offs_sb", [P, S // LIST_ROWS], U16)
+        kidx_sb = sb("kidx_sb", [P, S // LIST_ROWS], U16)
+        nb_sb = sb("nb_sb", [P, S // LIST_ROWS], U16)
+        d_table = at("d_table", [P, TABLE], U32, 4096)
+        x_table = sb("x_table", [P, TABLE], U32)
+        d_scale_table = at("d_scale_table", [P, TABLE], U8, 1024)
+        x_scale_table = sb("x_scale_table", [P, TABLE], U8)
+        w2_scale_raw = sb("w2_scale_raw", [P, S], U8)
+        gn_sb = sb("gn_sb", [P, PACK], F32)
+
+        nc.vector.memset(d_scale_table[:].bitcast(I32), 0)
+        nc.gpsimd.memset(x_scale_table[:].bitcast(I32), 0)
+        nc.vector.memset(w2_scale_raw[:].bitcast(I32), 0)
+
+        w1_rows = w1.rearrange("(p j) c -> p j c", j=PACK)
+        w1_raw = [sb("w1_raw%d" % a, [P, PACK, HALF], F32) for a in range(2)]
+        nc.sync.dma_start(kidx_sb[:], kidx)
+        nc.sync.dma_start(offs_sb[:], offs)
+        nc.sync.dma_start(nb_sb[:], nb)
+        nc.sync.dma_start(gn_sb[:], gn.rearrange("(p t) o -> p (t o)", t=PACK))
+        nc.sync.dma_start(d_table[:].bitcast(I32), words_of(d_words))
+        nc.sync.dma_start(w1_raw[0][:], w1_rows[:, :, cols(0, HALF)])
+        nc.sync.dma_start(x_table[:].bitcast(I32), words_of(x_words))
+        nc.sync.dma_start(w1_raw[1][:], w1_rows[:, :, cols(1, HALF)])
+        ds = d_scales[0].bitcast(I32)
+        for e in range(2):
+            nc.scalar.dma_start(d_scale_table[e:P:16, :].bitcast(I32), ds[e:16:2, :])
+        xs = x_scales[0].bitcast(I32)
+        for q in range(4):
+            nc.gpsimd.dma_start(x_scale_table[32 * q : 32 * q + 4, :].bitcast(I32), xs[4 * q : 4 * q + 4, :])
+        ws = w2_scales[0].bitcast(I32)
+        for q in range(4):
+            nc.gpsimd.dma_start(w2_scale_raw[32 * q : 32 * q + 4, :].bitcast(I32), ws[4 * q : 4 * q + 4, :])
+
+        warm = sb("warm", [P, PACK], F32)
+        nc.scalar.activation(warm[:], gn_sb[:], GELU)
+
+        d_scale_picked = sb("d_scale_picked", [P, S], U8)
+        nc.vector.tensor_copy(d_scale_picked[:], d_scale_table[:].indirect(kidx_sb[:]))
+        d_scale = sb("d_scale", [P, S], U8)
+        deal(d_scale[:], d_scale_picked[:])
+        for e in range(2):
+            nc.scalar.dma_start(d_scale[2 + e : P : 32, :].bitcast(I32), d_scale[16 + e : P : 32, :].bitcast(I32))
+        d_picked = at("d_picked", [P, S], U32, 0)
+        nc.vector.tensor_copy(d_picked[:], d_table[:].indirect(kidx_sb[:]))
+        w2_raw = at("w2_raw", [P, S], I32, 4096)
+        nc.sync.dma_start(w2_raw[:], words_of(w2_words))
+        res_sb = at("res_sb", [P, PACK, S], F32, 6144)
+        nc.sync.dma_start(res_sb[:], res.rearrange("(p t) j -> p t j", t=PACK))
+        d_codes = sb("d_codes", [P, S], U32)
+        deal(d_codes[:].bitcast(I32), d_picked[:].bitcast(I32))
+
+        x_scale = at("x_scale", [P, S], U8, 2048)
+        nc.vector.tensor_copy(x_scale[:], x_scale_table[:].indirect(offs_sb[:]))
+        x_codes = sb("x_codes", [P, S], U32, tag="x_scale_table")
+        for a in range(2):
+            nc.vector.tensor_copy(x_codes[:, cols(a, HALF)], x_table[:].indirect(entries(offs_sb, a, HALF)))
+
+        def product(bank, t, w_codes, w_scale, codes, scale, j):
+            nc.tensor.matmul_mx(
+                out=bank,
+                lhsT=w_codes[:, cols(t, P)].bitcast(FP8X4),
+                lhsT_scale=w_scale[:, cols(t, P)],
+                rhs=codes[:, j].bitcast(FP8X4),
+                rhs_scale=scale[:, j],
+                start=True,
+                stop=True,
+            )
+
+        def quantise(codes, scale, j, values):
+            nc.vector.quantize_mx(out=codes[:, j].bitcast(FP8X4), scales=scale[:, j], in_=values)
+
+        w1_bf = sb("w1_bf", [P, PACK * P * PACK], BF16)
+        w1_view = w1_bf[:].rearrange("p (t m j) -> p m j t", t=PACK, j=PACK)
+        for a in range(2):
+            nc.scalar.copy(
+                w1_view[:, cols(a, HALF // PACK)], w1_raw[a][:].rearrange("p j (m t) -> p m j t", t=PACK)
+            )
+
+        z_codes = sb("z_codes", [P, S], U32)
+        z_scale = sb("z_scale", [P, S], U8)
+        gn_spread = gn_sb[:].unsqueeze(1).to_broadcast([P, CHUNK, PACK])
+        z_bf = []
+        for c in range(CHUNKS):
+            bank = psum.tile([P, PACK, CHUNK], F32, name="chunk_bank%d" % c)
+            for t in range(PACK):
+                product(bank[:, t, :], t, d_codes, d_scale, x_codes, x_scale, cols(c, CHUNK))
+            zc = sb("z_bf%d" % c, [P, CHUNK * PACK], BF16)
+            nc.vector.scalar_tensor_tensor(
+                out=zc[:].rearrange("p (n t) -> p n t", t=PACK),
+                in0=bank[:].rearrange("p t n -> p n t"),
+                scalar=0.0625,
+                in1=gn_spread,
+                op0=MULT,
+                op1=MULT,
+            )
+            z_bf.append(zc)
+            if c > 0:
+                quantise(z_codes, z_scale, cols(c - 1, CHUNK), z_bf[c - 1][:])
+        w1_codes = sb("w1_codes", [P, S], U32)
+        w1_scale = sb("w1_scale", [P, S], U8)
+        quantise(w1_codes, w1_scale, cols(0, P), w1_bf[:, cols(0, P * PACK)])
+        quantise(z_codes, z_scale, cols(CHUNKS - 1, CHUNK), z_bf[CHUNKS - 1][:])
+        for t in range(1, PACK):
+            quantise(w1_codes, w1_scale, cols(t, P), w1_bf[:, cols(t, P * PACK)])
+
+        w2_codes = sb("w2_codes", [P, S], U32)
+        deal(w2_codes[:].bitcast(I32), w2_raw[:])
+        w2_scale = sb("w2_scale", [P, S], U8)
+        deal(w2_scale[:], w2_scale_raw[:])
+
+        z2 = [sb("z2_%d" % a, [P, PACK, HALF], F32) for a in range(2)]
+        hidden_banks = []
+        h_window = []
+        h_plain = []
+
+        def plain_copy(t, j):
+            nc.scalar.activation(h_plain[t][:, j], hidden_banks[t][:, j], GELU)
+
+        def add_neighbours(t, c, width):
+            a, first = divmod(c * width, HALF)
+            nc.vector.tensor_tensor(
+                z2[a][:, t, first : first + width],
+                h_window[t][:].indirect(entries(nb_sb, c, width)),
+                h_plain[t][:, cols(c, width)],
+                ADD,
+            )
+
+        for t in range(PACK):
+            bank = psum.tile([P, S], F32, name="hidden_bank%d" % t)
+            for a in range(2):
+                product(bank[:, cols(a, HALF)], t, w1_codes, w1_scale, z_codes, z_scale, cols(a, HALF))
+            hidden_banks.append(bank)
+            h_window.append(sb("h_window%d" % t, [P, S], F32))
+            h_plain.append(sb("h_plain%d" % t, [P, S], F32))
+            nc.scalar.activation(h_window[t][:], bank[:], GELU)
+            if t < 2:
+                plain_copy(t, slice(0, S))
+                add_neighbours(t, 0, HALF)
+                add_neighbours(t, 1, HALF)
+            else:
+                plain_copy(t, cols(0, HALF))
+        add_neighbours(2, 0, HALF)
+        add_neighbours(3, 0, CHUNK)
+        add_neighbours(3, 1, CHUNK)
+        plain_copy(2, cols(1, HALF))
+        plain_copy(3, cols(1, HALF))
+        add_neighbours(2, 1, HALF)
+        add_neighbours(3, 2, CHUNK)
+        add_neighbours(3, 3, CHUNK)
+
+        z2_codes = sb("z2_codes", [P, S], U32)
+        z2_scale = sb("z2_scale", [P, S], U8)
+        y_codes = sb("y_codes", [P, S], U32)
+        y_scale = sb("y_scale", [P, S], U8)
+        out_rows = out_0.rearrange("(p t) j -> p t j", t=PACK)
+        banks = []
+        for c in range(CHUNKS):
+            zb = sb("z2_bf%d" % c, [P, CHUNK * PACK], BF16)
+            source = z2[c // 2][:, :, cols(c % 2, CHUNK)]
+            nc.scalar.copy(
+                zb[:].rearrange("p (g i t) -> p g t i", i=4, t=PACK), source.rearrange("p t (g i) -> p g t i", i=4)
+            )
+            quantise(z2_codes, z2_scale, cols(c, CHUNK), zb[:])
+            bank = psum.tile([P, PACK, CHUNK], F32, name="chunk_bank%d" % c)
+            for t in range(PACK):
+                product(bank[:, t, :], t, w2_codes, w2_scale, z2_codes, z2_scale, cols(c, CHUNK))
+            banks.append(bank)
+        y_bf = []
+        for c in range(CHUNKS):
+            y = sb("y%d" % c, [P, PACK, CHUNK], F32)
+            nc.vector.tensor_tensor(y[:], banks[c][:], res_sb[:, :, cols(c, CHUNK)], ADD)
+            nc.sync.dma_start(out_rows[:, :, cols(c, CHUNK)], y[:])
+            yb = sb("y_bf%d" % c, [P, CHUNK * PACK], BF16)
+            nc.scalar.copy(
+                yb[:].rearrange("p (g i t) -> p g t i", i=4, t=PACK), y[:].rearrange("p t (g i) -> p g t i", i=4)
+            )
+            y_bf.append(yb)
+        out_words = words_of(out_1)
+        for c in range(CHUNKS):
+            quantise(y_codes, y_scale, cols(c, CHUNK), y_bf[c][:])
+            if c % 2 == 1:
+                nc.sync.dma_start(out_words[:, cols(c // 2, HALF)], y_codes[:, cols(c // 2, HALF)].bitcast(I32))
+        out_scales = out_2[0].bitcast(I32)
+        for q in range(4):
+            queue = nc.scalar if q % 2 else nc.sync
+            queue.dma_start(out_scales[4 * q : 4 * q + 4, :], y_scale[32 * q : 32 * q + 4, :].bitcast(I32))

@@ -56,39 +56,34 @@ def tile_picked_scoremlp_gelu_po_kernel(
         offs_sb = sb("offs_sb", [P, S // LIST_ROWS], U16)
         kidx_sb = sb("kidx_sb", [P, S // LIST_ROWS], U16)
         nb_sb = sb("nb_sb", [P, S // LIST_ROWS], U16)
-        d_table = at("d_table", [P, TABLE], U32, 4096)
-        x_table = sb("x_table", [P, TABLE], U32)
-        d_scale_table = at("d_scale_table", [P, TABLE], U8, 1024)
+        d_scale_table = sb("d_scale_table", [P, TABLE], U8)
         x_scale_table = sb("x_scale_table", [P, TABLE], U8)
-        w2_scale_raw = sb("w2_scale_raw", [P, S], U8)
         gn_sb = sb("gn_sb", [P, PACK], F32)
 
         nc.vector.memset(d_scale_table[:].bitcast(I32), 0)
+        warm = at("warm", [P, 32], F32, 8128)
+        nc.gpsimd.memset(warm[:], 0.0)
         nc.gpsimd.memset(x_scale_table[:].bitcast(I32), 0)
-        nc.vector.memset(w2_scale_raw[:].bitcast(I32), 0)
 
         w1_rows = w1.rearrange("(p j) c -> p j c", j=PACK)
-        w1_raw = [sb("w1_raw%d" % a, [P, PACK, HALF], F32) for a in range(2)]
+        w1_raw = [sb("w1_raw0", [P, PACK, HALF], F32)]
+        nc.sync.dma_start(gn_sb[:], gn.rearrange("(p t) o -> p (t o)", t=PACK))
         nc.sync.dma_start(kidx_sb[:], kidx)
         nc.sync.dma_start(offs_sb[:], offs)
         nc.sync.dma_start(nb_sb[:], nb)
-        nc.sync.dma_start(gn_sb[:], gn.rearrange("(p t) o -> p (t o)", t=PACK))
-        nc.sync.dma_start(d_table[:].bitcast(I32), words_of(d_words))
         nc.sync.dma_start(w1_raw[0][:], w1_rows[:, :, cols(0, HALF)])
-        nc.sync.dma_start(x_table[:].bitcast(I32), words_of(x_words))
-        nc.sync.dma_start(w1_raw[1][:], w1_rows[:, :, cols(1, HALF)])
         ds = d_scales[0].bitcast(I32)
         for e in range(2):
-            nc.scalar.dma_start(d_scale_table[e:P:16, :].bitcast(I32), ds[e:16:2, :])
+            nc.sync.dma_start(d_scale_table[e:P:16, :].bitcast(I32), ds[e:16:2, :])
         xs = x_scales[0].bitcast(I32)
         for q in range(4):
-            nc.gpsimd.dma_start(x_scale_table[32 * q : 32 * q + 4, :].bitcast(I32), xs[4 * q : 4 * q + 4, :])
-        ws = w2_scales[0].bitcast(I32)
-        for q in range(4):
-            nc.gpsimd.dma_start(w2_scale_raw[32 * q : 32 * q + 4, :].bitcast(I32), ws[4 * q : 4 * q + 4, :])
+            nc.sync.dma_start(x_scale_table[32 * q : 32 * q + 4, :].bitcast(I32), xs[4 * q : 4 * q + 4, :])
 
-        warm = sb("warm", [P, PACK], F32)
-        nc.scalar.activation(warm[:], gn_sb[:], GELU)
+        nc.scalar.activation(warm[:], warm[:], GELU)
+        d_table = at("d_table", [P, TABLE], U32, 0)
+        x_table = at("x_table", [P, TABLE], U32, 8192)
+        nc.sync.dma_start(d_table[:].bitcast(I32), words_of(d_words))
+        nc.sync.dma_start(x_table[:].bitcast(I32), words_of(x_words))
 
         d_scale_picked = sb("d_scale_picked", [P, S], U8)
         nc.vector.tensor_copy(d_scale_picked[:], d_scale_table[:].indirect(kidx_sb[:]))
@@ -96,18 +91,25 @@ def tile_picked_scoremlp_gelu_po_kernel(
         deal(d_scale[:], d_scale_picked[:])
         for e in range(2):
             nc.scalar.dma_start(d_scale[2 + e : P : 32, :].bitcast(I32), d_scale[16 + e : P : 32, :].bitcast(I32))
-        d_picked = at("d_picked", [P, S], U32, 0)
+        w1_raw.append(sb("w1_raw1", [P, PACK, HALF], F32, tag="d_scale_picked"))
+        nc.sync.dma_start(w1_raw[1][:], w1_rows[:, :, cols(1, HALF)])
+        x_scale = sb("x_scale", [P, S], U8)
+        nc.vector.tensor_copy(x_scale[:], x_scale_table[:].indirect(offs_sb[:]))
+        d_picked = sb("d_picked", [P, S], U32)
         nc.vector.tensor_copy(d_picked[:], d_table[:].indirect(kidx_sb[:]))
-        w2_raw = at("w2_raw", [P, S], I32, 4096)
+        w2_raw = at("w2_raw", [P, S], I32, 0)
         nc.sync.dma_start(w2_raw[:], words_of(w2_words))
-        res_sb = at("res_sb", [P, PACK, S], F32, 6144)
-        nc.sync.dma_start(res_sb[:], res.rearrange("(p t) j -> p t j", t=PACK))
+        w2_scale_raw = at("w2_scale_raw", [P, S], U8, 2048)
+        nc.vector.memset(w2_scale_raw[:].bitcast(I32), 0)
+        ws = w2_scales[0].bitcast(I32)
+        for q in range(4):
+            nc.sync.dma_start(w2_scale_raw[32 * q : 32 * q + 4, :].bitcast(I32), ws[4 * q : 4 * q + 4, :])
         d_codes = sb("d_codes", [P, S], U32)
         deal(d_codes[:].bitcast(I32), d_picked[:].bitcast(I32))
+        res_sb = sb("res_sb", [P, PACK, S], F32, tag="d_picked")
+        nc.sync.dma_start(res_sb[:], res.rearrange("(p t) j -> p t j", t=PACK))
 
-        x_scale = at("x_scale", [P, S], U8, 2048)
-        nc.vector.tensor_copy(x_scale[:], x_scale_table[:].indirect(offs_sb[:]))
-        x_codes = sb("x_codes", [P, S], U32, tag="x_scale_table")
+        x_codes = sb("x_codes", [P, S], U32)
         for a in range(2):
             nc.vector.tensor_copy(x_codes[:, cols(a, HALF)], x_table[:].indirect(entries(offs_sb, a, HALF)))
 
@@ -135,36 +137,39 @@ def tile_picked_scoremlp_gelu_po_kernel(
         z_codes = sb("z_codes", [P, S], U32)
         z_scale = sb("z_scale", [P, S], U8)
         gn_spread = gn_sb[:].unsqueeze(1).to_broadcast([P, CHUNK, PACK])
-        z_bf = []
+        z_bf = sb("z_bf", [P, S * PACK], BF16)
+        w1_codes = sb("w1_codes", [P, S], U32)
+        w1_scale = sb("w1_scale", [P, S], U8)
+
+        def quantise_cols(codes, scale, values, first, width):
+            quantise(codes, scale, slice(first, first + width), values[:, first * PACK : (first + width) * PACK])
+
         for c in range(CHUNKS):
             bank = psum.tile([P, PACK, CHUNK], F32, name="chunk_bank%d" % c)
             for t in range(PACK):
                 product(bank[:, t, :], t, d_codes, d_scale, x_codes, x_scale, cols(c, CHUNK))
-            zc = sb("z_bf%d" % c, [P, CHUNK * PACK], BF16)
             nc.vector.scalar_tensor_tensor(
-                out=zc[:].rearrange("p (n t) -> p n t", t=PACK),
+                out=z_bf[:, cols(c, CHUNK * PACK)].rearrange("p (n t) -> p n t", t=PACK),
                 in0=bank[:].rearrange("p t n -> p n t"),
                 scalar=0.0625,
                 in1=gn_spread,
                 op0=MULT,
                 op1=MULT,
             )
-            z_bf.append(zc)
-            if c > 0:
-                quantise(z_codes, z_scale, cols(c - 1, CHUNK), z_bf[c - 1][:])
-        w1_codes = sb("w1_codes", [P, S], U32)
-        w1_scale = sb("w1_scale", [P, S], U8)
-        quantise(w1_codes, w1_scale, cols(0, P), w1_bf[:, cols(0, P * PACK)])
-        quantise(z_codes, z_scale, cols(CHUNKS - 1, CHUNK), z_bf[CHUNKS - 1][:])
-        for t in range(1, PACK):
-            quantise(w1_codes, w1_scale, cols(t, P), w1_bf[:, cols(t, P * PACK)])
+            if c == 2:
+                quantise_cols(z_codes, z_scale, z_bf, 0, HALF)
+        quantise_cols(w1_codes, w1_scale, w1_bf, 0, P)
+        quantise_cols(z_codes, z_scale, z_bf, 2 * CHUNK, CHUNK)
+        quantise_cols(z_codes, z_scale, z_bf, 3 * CHUNK, CHUNK)
+        quantise_cols(w1_codes, w1_scale, w1_bf, P, P)
+        quantise_cols(w1_codes, w1_scale, w1_bf, 2 * P, 2 * P)
 
         w2_codes = sb("w2_codes", [P, S], U32)
         deal(w2_codes[:].bitcast(I32), w2_raw[:])
         w2_scale = sb("w2_scale", [P, S], U8)
         deal(w2_scale[:], w2_scale_raw[:])
 
-        z2 = [sb("z2_%d" % a, [P, PACK, HALF], F32) for a in range(2)]
+        z2 = [at("z2_0", [P, PACK, HALF], F32, 0), sb("z2_1", [P, PACK, HALF], F32)]
         hidden_banks = []
         h_window = []
         h_plain = []
@@ -183,8 +188,9 @@ def tile_picked_scoremlp_gelu_po_kernel(
 
         for t in range(PACK):
             bank = psum.tile([P, S], F32, name="hidden_bank%d" % t)
-            for a in range(2):
-                product(bank[:, cols(a, HALF)], t, w1_codes, w1_scale, z_codes, z_scale, cols(a, HALF))
+            pieces = (cols(0, HALF), cols(2, CHUNK), cols(3, CHUNK)) if t == 0 else (slice(0, S),)
+            for j in pieces:
+                product(bank[:, j], t, w1_codes, w1_scale, z_codes, z_scale, j)
             hidden_banks.append(bank)
             h_window.append(sb("h_window%d" % t, [P, S], F32))
             h_plain.append(sb("h_plain%d" % t, [P, S], F32))
@@ -193,49 +199,69 @@ def tile_picked_scoremlp_gelu_po_kernel(
                 plain_copy(t, slice(0, S))
                 add_neighbours(t, 0, HALF)
                 add_neighbours(t, 1, HALF)
-            else:
+            elif t == 2:
                 plain_copy(t, cols(0, HALF))
-        add_neighbours(2, 0, HALF)
-        add_neighbours(3, 0, CHUNK)
-        add_neighbours(3, 1, CHUNK)
-        plain_copy(2, cols(1, HALF))
-        plain_copy(3, cols(1, HALF))
-        add_neighbours(2, 1, HALF)
-        add_neighbours(3, 2, CHUNK)
-        add_neighbours(3, 3, CHUNK)
-
+            else:
+                plain_copy(t, cols(0, CHUNK))
+                plain_copy(t, cols(1, CHUNK))
         z2_codes = sb("z2_codes", [P, S], U32)
         z2_scale = sb("z2_scale", [P, S], U8)
         y_codes = sb("y_codes", [P, S], U32)
         y_scale = sb("y_scale", [P, S], U8)
         out_rows = out_0.rearrange("(p t) j -> p t j", t=PACK)
-        banks = []
-        for c in range(CHUNKS):
-            zb = sb("z2_bf%d" % c, [P, CHUNK * PACK], BF16)
-            source = z2[c // 2][:, :, cols(c % 2, CHUNK)]
-            nc.scalar.copy(
-                zb[:].rearrange("p (g i t) -> p g t i", i=4, t=PACK), source.rearrange("p t (g i) -> p g t i", i=4)
-            )
-            quantise(z2_codes, z2_scale, cols(c, CHUNK), zb[:])
-            bank = psum.tile([P, PACK, CHUNK], F32, name="chunk_bank%d" % c)
-            for t in range(PACK):
-                product(bank[:, t, :], t, w2_codes, w2_scale, z2_codes, z2_scale, cols(c, CHUNK))
-            banks.append(bank)
-        y_bf = []
-        for c in range(CHUNKS):
-            y = sb("y%d" % c, [P, PACK, CHUNK], F32)
-            nc.vector.tensor_tensor(y[:], banks[c][:], res_sb[:, :, cols(c, CHUNK)], ADD)
-            nc.sync.dma_start(out_rows[:, :, cols(c, CHUNK)], y[:])
-            yb = sb("y_bf%d" % c, [P, CHUNK * PACK], BF16)
-            nc.scalar.copy(
-                yb[:].rearrange("p (g i t) -> p g t i", i=4, t=PACK), y[:].rearrange("p t (g i) -> p g t i", i=4)
-            )
-            y_bf.append(yb)
         out_words = words_of(out_1)
-        for c in range(CHUNKS):
-            quantise(y_codes, y_scale, cols(c, CHUNK), y_bf[c][:])
-            if c % 2 == 1:
-                nc.sync.dma_start(out_words[:, cols(c // 2, HALF)], y_codes[:, cols(c // 2, HALF)].bitcast(I32))
+        z2_bf = [sb("z2_bf%d" % c, [P, CHUNK * PACK], BF16) for c in range(CHUNKS)]
+        y = [sb("y%d" % c, [P, PACK, CHUNK], F32) for c in range(CHUNKS)]
+        y_bf = sb("y_bf", [P, S * PACK], BF16)
+        out_banks = [psum.tile([P, PACK, CHUNK], F32, name="chunk_bank%d" % c) for c in range(CHUNKS)]
+
+        def weave(copy, woven, slots):
+            copy(woven.rearrange("p (g i t) -> p g t i", i=4, t=PACK), slots.rearrange("p t (g i) -> p g t i", i=4))
+
+        def round_z2(c):
+            weave(nc.scalar.copy, z2_bf[c][:], z2[c // 2][:, :, cols(c % 2, CHUNK)])
+
+        def second_layer(c):
+            quantise(z2_codes, z2_scale, cols(c, CHUNK), z2_bf[c][:])
+            for t in range(PACK):
+                product(out_banks[c][:, t, :], t, w2_codes, w2_scale, z2_codes, z2_scale, cols(c, CHUNK))
+
+        def add_residual(c):
+            nc.vector.tensor_tensor(y[c][:], out_banks[c][:], res_sb[:, :, cols(c, CHUNK)], ADD)
+            nc.sync.dma_start(out_rows[:, :, cols(c, CHUNK)], y[c][:])
+
+        def round_y(c, copy):
+            weave(copy, y_bf[:, cols(c, CHUNK * PACK)], y[c][:])
+
+        def store_codes(a):
+            nc.sync.dma_start(out_words[:, cols(a, HALF)], y_codes[:, cols(a, HALF)].bitcast(I32))
+
+        add_neighbours(2, 0, HALF)
+        add_neighbours(3, 0, CHUNK)
+        add_neighbours(3, 1, CHUNK)
+        plain_copy(2, cols(1, HALF))
+        add_neighbours(2, 1, HALF)
+        round_z2(0)
+        second_layer(0)
+        plain_copy(3, cols(1, HALF))
+        add_neighbours(3, 2, CHUNK)
+        add_neighbours(3, 3, CHUNK)
+        round_z2(1)
+        second_layer(1)
+        for c in range(2):
+            add_residual(c)
+            round_z2(c + 2)
+            second_layer(c + 2)
+        for c in range(2):
+            round_y(c, nc.scalar.copy)
+            add_residual(c + 2)
+        quantise_cols(y_codes, y_scale, y_bf, 0, HALF)
+        store_codes(0)
+        round_y(2, nc.scalar.copy)
+        round_y(3, nc.vector.tensor_copy)
+        quantise_cols(y_codes, y_scale, y_bf, 2 * CHUNK, CHUNK)
+        quantise_cols(y_codes, y_scale, y_bf, 3 * CHUNK, CHUNK)
+        store_codes(1)
         out_scales = out_2[0].bitcast(I32)
         for q in range(4):
             queue = nc.scalar if q % 2 else nc.sync

from contextlib import ExitStack

import concourse.mybir as mybir

F32 = mybir.dt.float32
BF16 = mybir.dt.bfloat16
I32 = mybir.dt.int32
U32 = mybir.dt.uint32
U16 = mybir.dt.uint16
U8 = mybir.dt.uint8
FP8X4 = mybir.dt.float8_e4m3fn_x4
MULT = mybir.AluOpType.mult
ADD = mybir.AluOpType.add
GELU = mybir.ActivationFunctionType.Gelu_apprx_tanh

P = 128
PACK = 4
TABLE = 2048
S = 512
HALF = 256
CHUNK = 128
CHUNKS = S // CHUNK
LIST_ROWS = 16
FLOPS = 3 * 2 * 512 * 512 * 512


def tile_picked_scoremlp_gelu_po_kernel(
    tc, x_words, x_scales, d_words, d_scales, gn, w1, res, w2_words, w2_scales, offs, kidx, nb, out_0, out_1, out_2
):
    nc = tc.nc
    with ExitStack() as ctx:
        keep = ctx.enter_context(tc.tile_pool(name="keep", bufs=1))
        reuse = ctx.enter_context(tc.tile_pool(name="reuse", bufs=1))
        psum = ctx.enter_context(tc.psum_pool(name="psum", bufs=1))

        def sb(name, shape, dtype, tag=None):
            return keep.tile(shape, dtype, name=name, tag=tag or name, align_bytes=64)

        def at(name, shape, dtype, offset):
            return reuse.tile(shape, dtype, name=name, align_bytes=64, offset=offset)

        def words_of(packed):
            return packed[0].rearrange("p n t -> p (n t)").bitcast(I32)

        def deal(dealt, plain):
            nc.vector.tensor_copy(
                dealt.rearrange("p (t m) -> p m t", t=PACK), plain.rearrange("p (m t) -> p m t", t=PACK)
            )

        def cols(c, width):
            return slice(c * width, (c + 1) * width)

        def entries(lists, c, width):
            return lists[:, cols(c, width // LIST_ROWS)]

        offs_sb = sb("offs_sb", [P, S // LIST_ROWS], U16)
        kidx_sb = sb("kidx_sb", [P, S // LIST_ROWS], U16)
        nb_sb = sb("nb_sb", [P, S // LIST_ROWS], U16)
        d_scale_table = sb("d_scale_table", [P, TABLE], U8)
        x_scale_table = sb("x_scale_table", [P, TABLE], U8)
        gn_sb = sb("gn_sb", [P, PACK], F32)

        nc.vector.memset(d_scale_table[:].bitcast(I32), 0)
        warm = at("warm", [P, 32], F32, 8128)
        nc.gpsimd.memset(warm[:], 0.0)
        nc.gpsimd.memset(x_scale_table[:].bitcast(I32), 0)

        w1_rows = w1.rearrange("(p j) c -> p j c", j=PACK)
        w1_raw = [sb("w1_raw0", [P, PACK, HALF], F32)]
        nc.sync.dma_start(gn_sb[:], gn.rearrange("(p t) o -> p (t o)", t=PACK))
        nc.sync.dma_start(kidx_sb[:], kidx)
        nc.sync.dma_start(offs_sb[:], offs)
        nc.sync.dma_start(nb_sb[:], nb)
        nc.sync.dma_start(w1_raw[0][:], w1_rows[:, :, cols(0, HALF)])
        ds = d_scales[0].bitcast(I32)
        for e in range(2):
            nc.sync.dma_start(d_scale_table[e:P:16, :].bitcast(I32), ds[e:16:2, :])
        xs = x_scales[0].bitcast(I32)
        for q in range(4):
            nc.sync.dma_start(x_scale_table[32 * q : 32 * q + 4, :].bitcast(I32), xs[4 * q : 4 * q + 4, :])

        nc.scalar.activation(warm[:], warm[:], GELU)
        d_table = at("d_table", [P, TABLE], U32, 0)
        x_table = at("x_table", [P, TABLE], U32, 8192)
        nc.sync.dma_start(d_table[:].bitcast(I32), words_of(d_words))
        nc.sync.dma_start(x_table[:].bitcast(I32), words_of(x_words))

        d_scale_picked = sb("d_scale_picked", [P, S], U8)
        nc.vector.tensor_copy(d_scale_picked[:], d_scale_table[:].indirect(kidx_sb[:]))
        d_scale = sb("d_scale", [P, S], U8)
        deal(d_scale[:], d_scale_picked[:])
        for e in range(2):
            nc.scalar.dma_start(d_scale[2 + e : P : 32, :].bitcast(I32), d_scale[16 + e : P : 32, :].bitcast(I32))
        w1_raw.append(sb("w1_raw1", [P, PACK, HALF], F32, tag="d_scale_picked"))
        nc.sync.dma_start(w1_raw[1][:], w1_rows[:, :, cols(1, HALF)])
        x_scale = sb("x_scale", [P, S], U8)
        nc.vector.tensor_copy(x_scale[:], x_scale_table[:].indirect(offs_sb[:]))
        d_picked = sb("d_picked", [P, S], U32)
        nc.vector.tensor_copy(d_picked[:], d_table[:].indirect(kidx_sb[:]))
        w2_raw = at("w2_raw", [P, S], I32, 0)
        nc.sync.dma_start(w2_raw[:], words_of(w2_words))
        w2_scale_raw = at("w2_scale_raw", [P, S], U8, 2048)
        nc.vector.memset(w2_scale_raw[:].bitcast(I32), 0)
        ws = w2_scales[0].bitcast(I32)
        for q in range(4):
            nc.sync.dma_start(w2_scale_raw[32 * q : 32 * q + 4, :].bitcast(I32), ws[4 * q : 4 * q + 4, :])
        d_codes = sb("d_codes", [P, S], U32)
        deal(d_codes[:].bitcast(I32), d_picked[:].bitcast(I32))
        res_sb = sb("res_sb", [P, PACK, S], F32, tag="d_picked")
        nc.sync.dma_start(res_sb[:], res.rearrange("(p t) j -> p t j", t=PACK))

        x_codes = sb("x_codes", [P, S], U32)
        for a in range(2):
            nc.vector.tensor_copy(x_codes[:, cols(a, HALF)], x_table[:].indirect(entries(offs_sb, a, HALF)))

        def product(bank, t, w_codes, w_scale, codes, scale, j):
            nc.tensor.matmul_mx(
                out=bank,
                lhsT=w_codes[:, cols(t, P)].bitcast(FP8X4),
                lhsT_scale=w_scale[:, cols(t, P)],
                rhs=codes[:, j].bitcast(FP8X4),
                rhs_scale=scale[:, j],
                start=True,
                stop=True,
            )

        def quantise(codes, scale, j, values):
            nc.vector.quantize_mx(out=codes[:, j].bitcast(FP8X4), scales=scale[:, j], in_=values)

        w1_bf = sb("w1_bf", [P, PACK * P * PACK], BF16)
        w1_view = w1_bf[:].rearrange("p (t m j) -> p m j t", t=PACK, j=PACK)
        for a in range(2):
            nc.scalar.copy(
                w1_view[:, cols(a, HALF // PACK)], w1_raw[a][:].rearrange("p j (m t) -> p m j t", t=PACK)
            )

        z_codes = sb("z_codes", [P, S], U32)
        z_scale = sb("z_scale", [P, S], U8)
        gn_spread = gn_sb[:].unsqueeze(1).to_broadcast([P, CHUNK, PACK])
        z_bf = sb("z_bf", [P, S * PACK], BF16)
        w1_codes = sb("w1_codes", [P, S], U32)
        w1_scale = sb("w1_scale", [P, S], U8)

        def quantise_cols(codes, scale, values, first, width):
            quantise(codes, scale, slice(first, first + width), values[:, first * PACK : (first + width) * PACK])

        for c in range(CHUNKS):
            bank = psum.tile([P, PACK, CHUNK], F32, name="chunk_bank%d" % c)
            for t in range(PACK):
                product(bank[:, t, :], t, d_codes, d_scale, x_codes, x_scale, cols(c, CHUNK))
            nc.vector.scalar_tensor_tensor(
                out=z_bf[:, cols(c, CHUNK * PACK)].rearrange("p (n t) -> p n t", t=PACK),
                in0=bank[:].rearrange("p t n -> p n t"),
                scalar=0.0625,
                in1=gn_spread,
                op0=MULT,
                op1=MULT,
            )
            if c == 2:
                quantise_cols(z_codes, z_scale, z_bf, 0, HALF)
        quantise_cols(w1_codes, w1_scale, w1_bf, 0, P)
        quantise_cols(z_codes, z_scale, z_bf, 2 * CHUNK, CHUNK)
        quantise_cols(z_codes, z_scale, z_bf, 3 * CHUNK, CHUNK)
        quantise_cols(w1_codes, w1_scale, w1_bf, P, P)
        quantise_cols(w1_codes, w1_scale, w1_bf, 2 * P, 2 * P)

        w2_codes = sb("w2_codes", [P, S], U32)
        deal(w2_codes[:].bitcast(I32), w2_raw[:])
        w2_scale = sb("w2_scale", [P, S], U8)
        deal(w2_scale[:], w2_scale_raw[:])

        z2 = [at("z2_0", [P, PACK, HALF], F32, 0), sb("z2_1", [P, PACK, HALF], F32)]
        hidden_banks = []
        h_window = []
        h_plain = []

        def plain_copy(t, j):
            nc.scalar.activation(h_plain[t][:, j], hidden_banks[t][:, j], GELU)

        def add_neighbours(t, c, width):
            a, first = divmod(c * width, HALF)
            nc.vector.tensor_tensor(
                z2[a][:, t, first : first + width],
                h_window[t][:].indirect(entries(nb_sb, c, width)),
                h_plain[t][:, cols(c, width)],
                ADD,
            )

        for t in range(PACK):
            bank = psum.tile([P, S], F32, name="hidden_bank%d" % t)
            pieces = (cols(0, HALF), cols(2, CHUNK), cols(3, CHUNK)) if t == 0 else (slice(0, S),)
            for j in pieces:
                product(bank[:, j], t, w1_codes, w1_scale, z_codes, z_scale, j)
            hidden_banks.append(bank)
            h_window.append(sb("h_window%d" % t, [P, S], F32))
            h_plain.append(sb("h_plain%d" % t, [P, S], F32))
            nc.scalar.activation(h_window[t][:], bank[:], GELU)
            if t < 2:
                plain_copy(t, slice(0, S))
                add_neighbours(t, 0, HALF)
                add_neighbours(t, 1, HALF)
            elif t == 2:
                plain_copy(t, cols(0, HALF))
            else:
                plain_copy(t, cols(0, CHUNK))
                plain_copy(t, cols(1, CHUNK))
        z2_codes = sb("z2_codes", [P, S], U32)
        z2_scale = sb("z2_scale", [P, S], U8)
        y_codes = sb("y_codes", [P, S], U32)
        y_scale = sb("y_scale", [P, S], U8)
        out_rows = out_0.rearrange("(p t) j -> p t j", t=PACK)
        out_words = words_of(out_1)
        z2_bf = [sb("z2_bf%d" % c, [P, CHUNK * PACK], BF16) for c in range(CHUNKS)]
        y = [sb("y%d" % c, [P, PACK, CHUNK], F32) for c in range(CHUNKS)]
        y_bf = sb("y_bf", [P, S * PACK], BF16)
        out_banks = [psum.tile([P, PACK, CHUNK], F32, name="chunk_bank%d" % c) for c in range(CHUNKS)]

        def weave(copy, woven, slots):
            copy(woven.rearrange("p (g i t) -> p g t i", i=4, t=PACK), slots.rearrange("p t (g i) -> p g t i", i=4))

        def round_z2(c):
            weave(nc.scalar.copy, z2_bf[c][:], z2[c // 2][:, :, cols(c % 2, CHUNK)])

        def second_layer(c):
            quantise(z2_codes, z2_scale, cols(c, CHUNK), z2_bf[c][:])
            for t in range(PACK):
                product(out_banks[c][:, t, :], t, w2_codes, w2_scale, z2_codes, z2_scale, cols(c, CHUNK))

        def add_residual(c):
            nc.vector.tensor_tensor(y[c][:], out_banks[c][:], res_sb[:, :, cols(c, CHUNK)], ADD)
            nc.sync.dma_start(out_rows[:, :, cols(c, CHUNK)], y[c][:])

        def round_y(c, copy):
            weave(copy, y_bf[:, cols(c, CHUNK * PACK)], y[c][:])

        def store_codes(a):
            nc.sync.dma_start(out_words[:, cols(a, HALF)], y_codes[:, cols(a, HALF)].bitcast(I32))

        add_neighbours(2, 0, HALF)
        add_neighbours(3, 0, CHUNK)
        add_neighbours(3, 1, CHUNK)
        plain_copy(2, cols(1, HALF))
        add_neighbours(2, 1, HALF)
        round_z2(0)
        second_layer(0)
        plain_copy(3, cols(1, HALF))
        add_neighbours(3, 2, CHUNK)
        add_neighbours(3, 3, CHUNK)
        round_z2(1)
        second_layer(1)
        for c in range(2):
            add_residual(c)
            round_z2(c + 2)
            second_layer(c + 2)
        for c in range(2):
            round_y(c, nc.scalar.copy)
            add_residual(c + 2)
        quantise_cols(y_codes, y_scale, y_bf, 0, HALF)
        store_codes(0)
        round_y(2, nc.scalar.copy)
        round_y(3, nc.vector.tensor_copy)
        quantise_cols(y_codes, y_scale, y_bf, 2 * CHUNK, CHUNK)
        quantise_cols(y_codes, y_scale, y_bf, 3 * CHUNK, CHUNK)
        store_codes(1)
        out_scales = out_2[0].bitcast(I32)
        for q in range(4):
            queue = nc.scalar if q % 2 else nc.sync
            queue.dma_start(out_scales[4 * q : 4 * q + 4, :], y_scale[32 * q : 32 * q + 4, :].bitcast(I32))
